import numpy as np
import ml_dtypes


def mxq(x, axis, fmt="e4m3"):
    dtype, down = {"e4m3": (ml_dtypes.float8_e4m3fn, 7), "e5m2": (ml_dtypes.float8_e5m2, 14)}[fmt]
    v = np.moveaxis(np.asarray(x, np.float32).astype(ml_dtypes.bfloat16).astype(np.float64), axis, -1)
    blocks = v.reshape(v.shape[:-1] + (-1, 32))
    amax = np.abs(blocks).max(-1, keepdims=True)
    byte = np.maximum(np.where(amax > 0, np.frexp(amax)[1] - 1 + 127, 0) - down, 1)
    scale = np.exp2(byte - 127.0)
    codes = (blocks / scale).astype(np.float32).astype(dtype).astype(np.float64)
    return np.moveaxis((codes * scale).reshape(v.shape), -1, axis)


WIDE = False


def mx_kscale(k):
    if not WIDE:
        return np.ones(k)
    levels = np.array([10, -10, 5, -5, 0])
    if k % 512:
        return np.exp2(np.random.permutation(np.resize(levels, k // 32))).repeat(32)
    a = np.empty((k // 512, 16))
    for p in range(k // 512):
        a[p, :8] = np.random.permutation(np.resize(levels, 8))
        for g in range(8):
            far = levels[np.abs(levels - a[p, g]) >= 10]
            a[p, g + 8] = far[np.random.randint(len(far))]
    return np.exp2(a.ravel()).repeat(32)


BF16 = ml_dtypes.bfloat16


def bf(x):
    return np.asarray(x, np.float32).astype(BF16)


def f64(x):
    return np.asarray(x).astype(np.float64)


E2M1 = np.array([0.0, 0.5, 1.0, 1.5, 2.0, 3.0, 4.0, 6.0, -0.0, -0.5, -1.0, -1.5, -2.0, -3.0, -4.0, -6.0])


def pack_weight(w, fmt):
    k, n = w.shape
    w = f64(bf(w)).reshape(k // 32, 32, n)
    amax = np.abs(w).max(1)
    if fmt == "e4m3":
        byte = np.frexp(amax)[1] - 1 + 127 - 7
    else:
        mant, ex = np.frexp(amax / 6.0)
        byte = np.where(mant > 0.5, ex, ex - 1) + 127
    byte = np.clip(np.where(amax > 0, byte, 1), 1, 254)
    scaled = (w * np.exp2(127.0 - byte)[:, None, :]).reshape(k, n).astype(np.float32)
    by_word = np.ascontiguousarray(scaled.reshape(k // 512, 128, 4, n).transpose(0, 1, 3, 2))
    if fmt == "e4m3":
        words = by_word.astype(ml_dtypes.float8_e4m3fn).view(np.uint8)
    else:
        c = by_word.astype(ml_dtypes.float4_e2m1fn).view(np.uint8) & 0xF
        words = c[..., 0::2] | (c[..., 1::2] << 4)
    return np.ascontiguousarray(words), np.ascontiguousarray(byte.astype(np.uint8).reshape(k // 512, 16, n))


def unpack_weight(words, scales, fmt):
    g, p, n, _ = words.shape
    if fmt == "e4m3":
        vals = np.ascontiguousarray(words).view(ml_dtypes.float8_e4m3fn).astype(np.float64)
    else:
        nib = np.empty((g, p, n, 4), np.uint8)
        nib[..., 0::2] = words & 0xF
        nib[..., 1::2] = words >> 4
        vals = E2M1[nib]
    vals = vals * np.repeat(np.exp2(scales.astype(np.float64) - 127.0), 8, axis=1)[..., None]
    return vals.transpose(0, 1, 3, 2).reshape(g * 512, n)
def pack4(w):
    words, scales = pack_weight(w, "e2m1")
    return words.reshape(words.shape[0], 128, -1), scales


def unpack4(words, scales):
    return unpack_weight(words.reshape(words.shape[0], 128, -1, 2), scales, "e2m1")


M, K, R, B = 768, 2048, 512, 4


def setup_inputs():
    s = mx_kscale(K)
    flux = np.random.standard_normal((M, K)) * s
    scat = np.random.standard_normal((K, R * B)) / np.sqrt(K) / s[:, None]
    prompt = np.random.standard_normal((K, R)) / np.sqrt(K) / s[:, None]
    delayed = np.random.standard_normal((K, R)) / np.sqrt(K) / s[:, None]
    scat_words, scat_scales = pack4(scat)
    prompt_words, prompt_scales = pack_weight(prompt, "e4m3")
    return {"flux": bf(flux),
            "scat_words": scat_words, "scat_scales": scat_scales,
            "prompt_words": prompt_words, "prompt_scales": prompt_scales,
            "delayed": bf(delayed),
            "chi_prompt": bf(0.5 + np.random.random_sample((R, B))),
            "chi_delayed": bf(0.3 + np.random.random_sample((R, B)))}


def reference(flux, scat_words, scat_scales, prompt_words, prompt_scales, delayed, chi_prompt, chi_delayed):
    x = mxq(f64(flux), 1, "e4m3")
    scatter = x @ unpack4(scat_words, scat_scales)
    fp = x @ unpack_weight(prompt_words, prompt_scales, "e4m3")
    fd = x @ mxq(f64(delayed), 0, "e4m3")
    src = scatter.reshape(M, R, B) + f64(chi_prompt) * fp[:, :, None] + f64(chi_delayed) * fd[:, :, None]
    return src.reshape(M, R * B)

@@ -1,0 +1,407 @@
+from contextlib import ExitStack
+
+import concourse.mybir as mybir
+from concourse.masks import make_identity
+
+F32 = mybir.dt.float32
+BF16 = mybir.dt.bfloat16
+I32 = mybir.dt.int32
+U32 = mybir.dt.uint32
+U8 = mybir.dt.uint8
+FP8X4 = mybir.dt.float8_e4m3fn_x4
+FP4X4 = mybir.dt.float4_e2m1fn_x4
+MULT = mybir.AluOpType.mult
+ADD = mybir.AluOpType.add
+
+M, K, R, B = 768, 2048, 512, 4
+P = 128
+PACK = 4
+PASSES = K // (P * PACK)
+M_TILES = M // P
+HALVES = 2
+R_HALF = R // HALVES
+N_HALF = R_HALF * B
+BANK = 512
+UNITS = HALVES * M_TILES
+SORT_FROM = 6
+POOL_SIDES = [(u, 0) for u in (1, 3, 5, 7,)]
+
+FLOPS = 2 * M * K * (R * B + 2 * R)
+
+
+def tile_multigroup_neutron_source_s10_kernel(
+    tc, flux, scat_words, scat_scales, prompt_words, prompt_scales, delayed, chi_prompt, chi_delayed, out
+):
+    nc = tc.nc
+    with ExitStack() as ctx:
+        keep = ctx.enter_context(tc.tile_pool(name="keep", bufs=1))
+        stream = ctx.enter_context(tc.tile_pool(name="stream", bufs=2))
+        psum = ctx.enter_context(tc.psum_pool(name="psum", bufs=2))
+        ctx.enter_context(tc.manual_schedule())
+
+        def kept(name, shape, dtype):
+            return keep.tile(shape, dtype, name=name, align_bytes=64)
+
+        ident = kept("ident", [P, P], F32)
+        make_identity(nc, ident[:])
+
+        scat_plane = [kept("scat_plane%d" % h, [P, PASSES, N_HALF], U8) for h in range(HALVES)]
+        prompt_plane = kept("prompt_plane", [P, R], U8)
+        nc.vector.memset(scat_plane[0][:].rearrange("p g n -> p (g n)").bitcast(I32), 0)
+        nc.vector.memset(prompt_plane[:].bitcast(I32), 0)
+        nc.vector.memset(scat_plane[1][:].rearrange("p g n -> p (g n)").bitcast(I32), 0)
+
+        flux_raw = [None] + [kept("flux_raw%d" % m, [P, K], BF16) for m in range(1, M_TILES)]
+        flux_first = [kept("flux_first%d" % pair, [P, K // 2], BF16) for pair in range(2)]
+        flux_sorted = {}
+        scat_codes = [kept("scat_codes%d" % c, [P, PASSES, 2 * BANK], U8) for c in range(2 * HALVES)]
+        prompt_codes = [kept("prompt_codes%d" % h, [P, PASSES, R_HALF], U32) for h in range(HALVES)]
+        delayed_raw = [
+            [kept("delayed_raw%d_%d" % (h, g), [P, PACK, R_HALF], BF16) for g in range(PASSES)] for h in range(HALVES)
+        ]
+        chi_raw = [kept("chi_raw%d" % i, [P, HALVES, 2 * B], BF16) for i in range(2)]
+
+        def load_flux(m):
+            nc.sync.dma_start(out=flux_raw[m][:], in_=flux[m * P : (m + 1) * P, :])
+
+        def load_scat_scales(h):
+            rows = scat_scales.rearrange("g (q r) n -> r q g n", r=4)
+            for r in range(4):
+                nc.sync.dma_start(
+                    out=scat_plane[h][r:P:32, :, :].bitcast(I32),
+                    in_=rows[r][:, :, h * N_HALF : (h + 1) * N_HALF].bitcast(I32),
+                )
+
+        def load_scat_codes(c):
+            src = scat_words.rearrange("g p c -> p g c")[:, :, c * 2 * BANK : (c + 1) * 2 * BANK]
+            nc.sync.dma_start(out=scat_codes[c][:].bitcast(I32), in_=src.bitcast(I32))
+
+        def load_prompt_scales():
+            for q in range(4):
+                nc.sync.dma_start(
+                    out=prompt_plane[32 * q : 32 * q + 16, :].bitcast(I32),
+                    in_=prompt_scales[:, 4 * q : 4 * q + 4, :].bitcast(I32),
+                )
+
+        def load_prompt_codes(h):
+            src = prompt_words.rearrange("g p n t -> p g (n t)")[:, :, h * PACK * R_HALF : (h + 1) * PACK * R_HALF]
+            nc.sync.dma_start(out=prompt_codes[h][:].bitcast(I32), in_=src.bitcast(I32))
+
+        def load_delayed(h, g):
+            rows = delayed[g * P * PACK : (g + 1) * P * PACK, h * R_HALF : (h + 1) * R_HALF]
+            nc.sync.dma_start(out=delayed_raw[h][g][:], in_=rows.rearrange("(p j) w -> p j w", j=PACK))
+
+        for i, chi in enumerate((chi_prompt, chi_delayed)):
+            nc.scalar.dma_start(out=chi_raw[i][:], in_=chi.rearrange("(h p r) b -> p h (r b)", h=HALVES, r=2))
+        for pair in range(2):
+            nc.sync.dma_start(out=flux_first[pair][:], in_=flux[:P, pair * K // 2 : (pair + 1) * K // 2])
+        load_delayed(0, 0)
+        load_flux(1)
+        load_delayed(0, 1)
+        load_flux(2)
+        load_delayed(0, 2)
+        load_flux(3)
+        load_delayed(0, 3)
+        load_prompt_scales()
+        load_prompt_codes(0)
+        load_scat_scales(0)
+        load_scat_codes(0)
+        load_flux(4)
+        load_scat_codes(1)
+        load_flux(5)
+        load_delayed(1, 0)
+        load_delayed(1, 1)
+        load_delayed(1, 2)
+        load_delayed(1, 3)
+        load_prompt_codes(1)
+        load_scat_scales(1)
+        load_scat_codes(2)
+        load_scat_codes(3)
+
+        flux_codes = kept("flux_codes", [P, M_TILES * PASSES * P], U32)
+        flux_plane = kept("flux_plane", [P, M_TILES * PASSES * P], U8)
+        delayed_grouped = [kept("delayed_grouped%d" % h, [P, PASSES * R_HALF * PACK], BF16) for h in range(HALVES)]
+        delayed_codes = [kept("delayed_codes%d" % h, [P, PASSES * R_HALF], U32) for h in range(HALVES)]
+        delayed_plane = [kept("delayed_plane%d" % h, [P, PASSES * R_HALF], U8) for h in range(HALVES)]
+        chi_rows = [kept("chi_rows%d" % h, [P, 2, N_HALF], BF16) for h in range(HALVES)]
+
+        flux_grouped = kept("flux_grouped", [P, M_TILES * K], BF16)
+        fission_sum = {}
+        scatter_bank = {}
+        scatter_rows = {}
+        results = {}
+        fission_terms = {}
+        fission_bank = {}
+
+        def turn_flux(m):
+            for pair in range(PASSES // 2):
+                bank = psum.tile([P, 4, P], F32, name="turn_bank", bufs=2)
+                if m == 0:
+                    words = flux_first[pair][:].bitcast(F32)
+                elif m < SORT_FROM:
+                    words = flux_raw[m][:].bitcast(F32)[:, 512 * pair : 512 * (pair + 1)]
+                else:
+                    words = flux_sorted[m][:, 512 * pair : 512 * (pair + 1)]
+                for i in range(4):
+                    if m < SORT_FROM:
+                        first = 256 * (i // 2)
+                        source = words[:, first + i % 2 : first + 256 : 2]
+                    else:
+                        source = words[:, i * P : (i + 1) * P]
+                    nc.tensor.transpose(bank[:, i, :], source, ident[:])
+                nc.scalar.copy(
+                    out=flux_grouped[:, (2 * m + pair) * 1024 : (2 * m + pair + 1) * 1024]
+                    .bitcast(F32)
+                    .rearrange("p (g m u) -> p g m u", g=2, u=2),
+                    in_=bank[:].rearrange("p (g u) m -> p g m u", u=2),
+                )
+
+        def sort_flux(m):
+            ordered = stream.tile([P, K // 2], F32, name="flux_sorted", bufs=2)
+            nc.scalar.copy(
+                out=ordered[:].rearrange("p (g u c) -> p g u c", g=PASSES, u=2),
+                in_=flux_raw[m][:].bitcast(F32).rearrange("p (g c u) -> p g u c", g=PASSES, u=2),
+            )
+            flux_sorted[m] = ordered
+
+        def quantize_flux(first, count):
+            cols = slice(first * 2 * P, (first + count) * 2 * P)
+            nc.vector.quantize_mx(
+                out=flux_codes[:, cols].bitcast(FP8X4),
+                scales=flux_plane[:, cols],
+                in_=flux_grouped[:, first * 1024 : (first + count) * 1024],
+            )
+
+        def spread_chi(h):
+            for i in range(2):
+                bank = psum.tile([P, 4, P], F32, name="scatter_bank", bufs=4)
+                words = chi_raw[i][:, h, :].bitcast(F32)
+                for j in range(4):
+                    nc.tensor.transpose(bank[:, j, :], words[:, j : j + 1].to_broadcast([P, P]), ident[:])
+                nc.scalar.copy(
+                    out=chi_rows[h][:, i, :].bitcast(F32).rearrange("p (c j) -> p c j", j=4),
+                    in_=bank[:].rearrange("p j c -> p c j"),
+                )
+
+        def group_delayed(h, g, copy):
+            copy(
+                out=delayed_grouped[h][:, g * 1024 : (g + 1) * 1024].rearrange("p (c i t) -> p c t i", i=4, t=PACK),
+                in_=delayed_raw[h][g][:].rearrange("p t (c i) -> p c t i", i=4),
+            )
+
+        def quantize_delayed(h, first, count):
+            cols = slice(first * R_HALF, (first + count) * R_HALF)
+            nc.vector.quantize_mx(
+                out=delayed_codes[h][:, cols].bitcast(FP8X4),
+                scales=delayed_plane[h][:, cols],
+                in_=delayed_grouped[h][:, first * 1024 : (first + count) * 1024],
+            )
+
+        def product(acc, m, rhs, rhs_scale):
+            for g in range(PASSES):
+                cols = slice((m * PASSES + g) * P, (m * PASSES + g + 1) * P)
+                nc.tensor.matmul_mx(
+                    out=acc,
+                    lhsT=flux_codes[:, cols].bitcast(FP8X4),
+                    lhsT_scale=flux_plane[:, cols],
+                    rhs=rhs(g),
+                    rhs_scale=rhs_scale(g),
+                    start=(g == 0),
+                    stop=(g == PASSES - 1),
+                )
+
+        def scatter(u, side):
+            h, m = divmod(u, M_TILES)
+            bank = psum.tile([P, BANK], F32, name="scatter_bank", bufs=4)
+            product(
+                bank[:],
+                m,
+                lambda g: scat_codes[2 * h + side][:, g, :].bitcast(FP4X4),
+                lambda g: scat_plane[h][:, g, side * BANK : (side + 1) * BANK],
+            )
+            if (u, side) in POOL_SIDES:
+                scatter_rows[u] = stream.tile([P, BANK], F32, name="scatter_rows", bufs=8)
+                nc.scalar.copy(out=scatter_rows[u][:], in_=bank[:])
+            scatter_bank[u, side] = bank
+
+        def delayed_rates(u):
+            h, m = divmod(u, M_TILES)
+            fission_bank[u] = psum.tile([P, 2, R_HALF], F32, name="fission_bank", bufs=2)
+            product(
+                fission_bank[u][:, 1, :],
+                m,
+                lambda g: delayed_codes[h][:, g * R_HALF : (g + 1) * R_HALF].bitcast(FP8X4),
+                lambda g: delayed_plane[h][:, g * R_HALF : (g + 1) * R_HALF],
+            )
+
+        def prompt_rates(u):
+            h, m = divmod(u, M_TILES)
+            product(
+                fission_bank[u][:, 0, :],
+                m,
+                lambda g: prompt_codes[h][:, g, :].bitcast(FP8X4),
+                lambda g: prompt_plane[4 * g : P, h * R_HALF : (h + 1) * R_HALF],
+            )
+
+        def spread_rates(u, i):
+            term = stream.tile([P, N_HALF], F32, name="term", bufs=6)
+            nc.vector.tensor_tensor(
+                out=term[:].rearrange("p (r b) -> p r b", b=B),
+                in0=fission_bank[u][:, i, :].unsqueeze(2).to_broadcast([P, R_HALF, B]),
+                in1=chi_rows[u // M_TILES][:, i, :].rearrange("p (r b) -> p r b", b=B),
+                op=MULT,
+            )
+            fission_terms[u, i] = term
+
+        def add_terms(u):
+            both = stream.tile([P, N_HALF], F32, name="both", bufs=6)
+            nc.gpsimd.tensor_tensor(out=both[:], in0=fission_terms[u, 0][:], in1=fission_terms[u, 1][:], op=ADD)
+            fission_sum[u] = both
+
+        def finish(u, side):
+            h, m = divmod(u, M_TILES)
+            result = stream.tile([P, BANK], F32, name="result", bufs=10)
+            cols = slice(side * BANK, (side + 1) * BANK)
+            if (u, side) in POOL_SIDES:
+                nc.gpsimd.tensor_tensor(out=result[:], in0=scatter_rows[u][:], in1=fission_sum[u][:, cols], op=ADD)
+            else:
+                nc.vector.tensor_tensor(out=result[:], in0=scatter_bank[u, side][:], in1=fission_sum[u][:, cols], op=ADD)
+            first = h * N_HALF + side * BANK
+            nc.sync.dma_start(out=out[m * P : (m + 1) * P, first : first + BANK], in_=result[:])
+
+        spread_chi(0)
+        turn_flux(0)
+        quantize_flux(0, 1)
+        quantize_flux(1, 1)
+        group_delayed(0, 0, nc.vector.tensor_copy)
+        turn_flux(1)
+        quantize_delayed(0, 0, 1)
+        quantize_flux(2, 2)
+        group_delayed(0, 1, nc.vector.tensor_copy)
+        turn_flux(2)
+        quantize_delayed(0, 1, 1)
+        quantize_flux(4, 2)
+        group_delayed(0, 2, nc.vector.tensor_copy)
+        turn_flux(3)
+        quantize_delayed(0, 2, 1)
+        group_delayed(0, 3, nc.vector.tensor_copy)
+        quantize_flux(6, 2)
+        quantize_delayed(0, 3, 1)
+        delayed_rates(0)
+        prompt_rates(0)
+        spread_rates(0, 0)
+        spread_rates(0, 1)
+        add_terms(0)
+        delayed_rates(1)
+        prompt_rates(1)
+        turn_flux(4)
+        scatter(0, 0)
+        spread_rates(1, 0)
+        spread_rates(1, 1)
+        quantize_flux(8, 2)
+        add_terms(1)
+        delayed_rates(2)
+        prompt_rates(2)
+        turn_flux(5)
+        group_delayed(1, 0, nc.scalar.copy)
+        group_delayed(1, 1, nc.scalar.copy)
+        scatter(0, 1)
+        spread_rates(2, 0)
+        spread_rates(2, 1)
+        quantize_flux(10, 2)
+        add_terms(2)
+        finish(0, 0)
+        finish(0, 1)
+        delayed_rates(3)
+        prompt_rates(3)
+        spread_chi(1)
+        group_delayed(1, 2, nc.scalar.copy)
+        group_delayed(1, 3, nc.scalar.copy)
+        scatter(1, 0)
+        scatter(1, 1)
+        spread_rates(3, 0)
+        spread_rates(3, 1)
+        add_terms(3)
+        finish(1, 0)
+        finish(1, 1)
+        delayed_rates(4)
+        prompt_rates(4)
+        scatter(2, 0)
+        scatter(2, 1)
+        spread_rates(4, 0)
+        spread_rates(4, 1)
+        quantize_delayed(1, 0, 4)
+        add_terms(4)
+        finish(2, 0)
+        finish(2, 1)
+        delayed_rates(5)
+        prompt_rates(5)
+        scatter(3, 0)
+        scatter(3, 1)
+        spread_rates(5, 0)
+        spread_rates(5, 1)
+        add_terms(5)
+        finish(3, 0)
+        finish(3, 1)
+        delayed_rates(6)
+        prompt_rates(6)
+        scatter(4, 0)
+        scatter(4, 1)
+        spread_rates(6, 0)
+        spread_rates(6, 1)
+        add_terms(6)
+        finish(4, 0)
+        finish(4, 1)
+        delayed_rates(7)
+        prompt_rates(7)
+        scatter(5, 0)
+        scatter(5, 1)
+        spread_rates(7, 0)
+        spread_rates(7, 1)
+        add_terms(7)
+        finish(5, 0)
+        finish(5, 1)
+        delayed_rates(8)
+        prompt_rates(8)
+        scatter(6, 0)
+        scatter(6, 1)
+        spread_rates(8, 0)
+        spread_rates(8, 1)
+        add_terms(8)
+        finish(6, 0)
+        finish(6, 1)
+        delayed_rates(9)
+        prompt_rates(9)
+        scatter(7, 0)
+        scatter(7, 1)
+        spread_rates(9, 0)
+        spread_rates(9, 1)
+        add_terms(9)
+        finish(7, 0)
+        finish(7, 1)
+        delayed_rates(10)
+        prompt_rates(10)
+        scatter(8, 0)
+        scatter(8, 1)
+        spread_rates(10, 0)
+        spread_rates(10, 1)
+        add_terms(10)
+        finish(8, 0)
+        finish(8, 1)
+        delayed_rates(11)
+        prompt_rates(11)
+        scatter(9, 0)
+        scatter(9, 1)
+        spread_rates(11, 0)
+        spread_rates(11, 1)
+        add_terms(11)
+        finish(9, 0)
+        finish(9, 1)
+        scatter(10, 0)
+        scatter(10, 1)
+        scatter(11, 0)
+        scatter(11, 1)
+        finish(10, 0)
+        finish(10, 1)
+        finish(11, 0)
+        finish(11, 1)

@@ -23,8 +23,12 @@ R_HALF = R // HALVES
 N_HALF = R_HALF * B
 BANK = 512
 UNITS = HALVES * M_TILES
-SORT_FROM = 6
-POOL_SIDES = [(u, 0) for u in (1, 3, 5, 7,)]
+PASS_COLS = R_HALF * PACK
+HEAD_TILES = 2
+LAG = 2
+GPSIMD_UNITS = (1, 3, 5, 7)
+DELAYED_STEPS = (2, 3)
+NARROW = BANK // 4
 
 FLOPS = 2 * M * K * (R * B + 2 * R)
 
@@ -42,6 +46,15 @@ def tile_multigroup_neutron_source_s10_kernel(
         def kept(name, shape, dtype):
             return keep.tile(shape, dtype, name=name, align_bytes=64)
 
+        def turn_bank(shape):
+            return psum.tile(shape, F32, name="turn_bank", bufs=2)
+
+        def rate_bank(shape):
+            return psum.tile(shape, F32, name="rate_bank", bufs=2)
+
+        def side_bank(shape):
+            return psum.tile(shape, F32, name="side_bank", bufs=4)
+
         ident = kept("ident", [P, P], F32)
         make_identity(nc, ident[:])
 
@@ -51,9 +64,8 @@ def tile_multigroup_neutron_source_s10_kernel(
         nc.vector.memset(prompt_plane[:].bitcast(I32), 0)
         nc.vector.memset(scat_plane[1][:].rearrange("p g n -> p (g n)").bitcast(I32), 0)
 
-        flux_raw = [None] + [kept("flux_raw%d" % m, [P, K], BF16) for m in range(1, M_TILES)]
         flux_first = [kept("flux_first%d" % pair, [P, K // 2], BF16) for pair in range(2)]
-        flux_sorted = {}
+        flux_rest = {m: kept("flux_rest%d" % m, [P, K], BF16) for m in range(1, M_TILES)}
         scat_codes = [kept("scat_codes%d" % c, [P, PASSES, 2 * BANK], U8) for c in range(2 * HALVES)]
         prompt_codes = [kept("prompt_codes%d" % h, [P, PASSES, R_HALF], U32) for h in range(HALVES)]
         delayed_raw = [
@@ -62,7 +74,7 @@ def tile_multigroup_neutron_source_s10_kernel(
         chi_raw = [kept("chi_raw%d" % i, [P, HALVES, 2 * B], BF16) for i in range(2)]
 
         def load_flux(m):
-            nc.sync.dma_start(out=flux_raw[m][:], in_=flux[m * P : (m + 1) * P, :])
+            nc.sync.dma_start(out=flux_rest[m][:], in_=flux[m * P : (m + 1) * P, :])
 
         def load_scat_scales(h):
             rows = scat_scales.rearrange("g (q r) n -> r q g n", r=4)
@@ -72,7 +84,8 @@ def tile_multigroup_neutron_source_s10_kernel(
                     in_=rows[r][:, :, h * N_HALF : (h + 1) * N_HALF].bitcast(I32),
                 )
 
-        def load_scat_codes(c):
+        def load_scat_codes(h, side):
+            c = 2 * h + side
             src = scat_words.rearrange("g p c -> p g c")[:, :, c * 2 * BANK : (c + 1) * 2 * BANK]
             nc.sync.dma_start(out=scat_codes[c][:].bitcast(I32), in_=src.bitcast(I32))
 
@@ -87,94 +100,72 @@ def tile_multigroup_neutron_source_s10_kernel(
             src = prompt_words.rearrange("g p n t -> p g (n t)")[:, :, h * PACK * R_HALF : (h + 1) * PACK * R_HALF]
             nc.sync.dma_start(out=prompt_codes[h][:].bitcast(I32), in_=src.bitcast(I32))
 
-        def load_delayed(h, g):
-            rows = delayed[g * P * PACK : (g + 1) * P * PACK, h * R_HALF : (h + 1) * R_HALF]
-            nc.sync.dma_start(out=delayed_raw[h][g][:], in_=rows.rearrange("(p j) w -> p j w", j=PACK))
+        def load_delayed(h, passes):
+            for g in passes:
+                rows = delayed[g * P * PACK : (g + 1) * P * PACK, h * R_HALF : (h + 1) * R_HALF]
+                nc.sync.dma_start(out=delayed_raw[h][g][:], in_=rows.rearrange("(p t) w -> p t w", t=PACK))
 
         for i, chi in enumerate((chi_prompt, chi_delayed)):
             nc.scalar.dma_start(out=chi_raw[i][:], in_=chi.rearrange("(h p r) b -> p h (r b)", h=HALVES, r=2))
         for pair in range(2):
             nc.sync.dma_start(out=flux_first[pair][:], in_=flux[:P, pair * K // 2 : (pair + 1) * K // 2])
-        load_delayed(0, 0)
+        load_delayed(0, (0, 1))
         load_flux(1)
-        load_delayed(0, 1)
-        load_flux(2)
-        load_delayed(0, 2)
-        load_flux(3)
-        load_delayed(0, 3)
+        load_delayed(0, (2, 3))
         load_prompt_scales()
         load_prompt_codes(0)
+        load_flux(2)
+        load_flux(3)
         load_scat_scales(0)
-        load_scat_codes(0)
         load_flux(4)
-        load_scat_codes(1)
+        load_scat_codes(0, 0)
         load_flux(5)
-        load_delayed(1, 0)
-        load_delayed(1, 1)
-        load_delayed(1, 2)
-        load_delayed(1, 3)
+        load_scat_codes(0, 1)
+        load_delayed(1, range(PASSES))
         load_prompt_codes(1)
         load_scat_scales(1)
-        load_scat_codes(2)
-        load_scat_codes(3)
+        load_scat_codes(1, 0)
+        load_scat_codes(1, 1)
 
+        flux_grouped = kept("flux_grouped", [P, M_TILES * K], BF16)
         flux_codes = kept("flux_codes", [P, M_TILES * PASSES * P], U32)
         flux_plane = kept("flux_plane", [P, M_TILES * PASSES * P], U8)
-        delayed_grouped = [kept("delayed_grouped%d" % h, [P, PASSES * R_HALF * PACK], BF16) for h in range(HALVES)]
+        delayed_grouped = [kept("delayed_grouped%d" % h, [P, PASSES * PASS_COLS], BF16) for h in range(HALVES)]
         delayed_codes = [kept("delayed_codes%d" % h, [P, PASSES * R_HALF], U32) for h in range(HALVES)]
         delayed_plane = [kept("delayed_plane%d" % h, [P, PASSES * R_HALF], U8) for h in range(HALVES)]
         chi_rows = [kept("chi_rows%d" % h, [P, 2, N_HALF], BF16) for h in range(HALVES)]
 
-        flux_grouped = kept("flux_grouped", [P, M_TILES * K], BF16)
-        fission_sum = {}
-        scatter_bank = {}
-        scatter_rows = {}
-        results = {}
+        scatter_sums = {}
         fission_terms = {}
-        fission_bank = {}
+        fission_sum = {}
 
         def turn_flux(m):
             for pair in range(PASSES // 2):
-                bank = psum.tile([P, 4, P], F32, name="turn_bank", bufs=2)
+                bank = turn_bank([P, 4, P])
                 if m == 0:
                     words = flux_first[pair][:].bitcast(F32)
-                elif m < SORT_FROM:
-                    words = flux_raw[m][:].bitcast(F32)[:, 512 * pair : 512 * (pair + 1)]
                 else:
-                    words = flux_sorted[m][:, 512 * pair : 512 * (pair + 1)]
+                    words = flux_rest[m][:].bitcast(F32)[:, 4 * P * pair : 4 * P * (pair + 1)]
                 for i in range(4):
-                    if m < SORT_FROM:
-                        first = 256 * (i // 2)
-                        source = words[:, first + i % 2 : first + 256 : 2]
-                    else:
-                        source = words[:, i * P : (i + 1) * P]
-                    nc.tensor.transpose(bank[:, i, :], source, ident[:])
+                    g, e = divmod(i, 2)
+                    nc.tensor.transpose(bank[:, i, :], words[:, 2 * P * g + e : 2 * P * (g + 1) : 2], ident[:])
+                first = m * K + pair * K // 2
                 nc.scalar.copy(
-                    out=flux_grouped[:, (2 * m + pair) * 1024 : (2 * m + pair + 1) * 1024]
-                    .bitcast(F32)
-                    .rearrange("p (g m u) -> p g m u", g=2, u=2),
-                    in_=bank[:].rearrange("p (g u) m -> p g m u", u=2),
+                    out=flux_grouped[:, first : first + K // 2].bitcast(F32).rearrange("p (g s e) -> p g s e", g=2, e=2),
+                    in_=bank[:].rearrange("p (g e) s -> p g s e", e=2),
                 )
 
-        def sort_flux(m):
-            ordered = stream.tile([P, K // 2], F32, name="flux_sorted", bufs=2)
-            nc.scalar.copy(
-                out=ordered[:].rearrange("p (g u c) -> p g u c", g=PASSES, u=2),
-                in_=flux_raw[m][:].bitcast(F32).rearrange("p (g c u) -> p g u c", g=PASSES, u=2),
-            )
-            flux_sorted[m] = ordered
-
-        def quantize_flux(first, count):
-            cols = slice(first * 2 * P, (first + count) * 2 * P)
+        def quantize_flux(m):
+            cols = slice(m * PASSES * P, (m + 1) * PASSES * P)
             nc.vector.quantize_mx(
                 out=flux_codes[:, cols].bitcast(FP8X4),
                 scales=flux_plane[:, cols],
-                in_=flux_grouped[:, first * 1024 : (first + count) * 1024],
+                in_=flux_grouped[:, m * K : (m + 1) * K],
             )
 
         def spread_chi(h):
             for i in range(2):
-                bank = psum.tile([P, 4, P], F32, name="scatter_bank", bufs=4)
+                bank = side_bank([P, 4, P])
                 words = chi_raw[i][:, h, :].bitcast(F32)
                 for j in range(4):
                     nc.tensor.transpose(bank[:, j, :], words[:, j : j + 1].to_broadcast([P, P]), ident[:])
@@ -185,7 +176,9 @@ def tile_multigroup_neutron_source_s10_kernel(
 
         def group_delayed(h, g, copy):
             copy(
-                out=delayed_grouped[h][:, g * 1024 : (g + 1) * 1024].rearrange("p (c i t) -> p c t i", i=4, t=PACK),
+                out=delayed_grouped[h][:, g * PASS_COLS : (g + 1) * PASS_COLS].rearrange(
+                    "p (c i t) -> p c t i", i=4, t=PACK
+                ),
                 in_=delayed_raw[h][g][:].rearrange("p t (c i) -> p c t i", i=4),
             )
 
@@ -194,7 +187,7 @@ def tile_multigroup_neutron_source_s10_kernel(
             nc.vector.quantize_mx(
                 out=delayed_codes[h][:, cols].bitcast(FP8X4),
                 scales=delayed_plane[h][:, cols],
-                in_=delayed_grouped[h][:, first * 1024 : (first + count) * 1024],
+                in_=delayed_grouped[h][:, first * PASS_COLS : (first + count) * PASS_COLS],
             )
 
         def product(acc, m, rhs, rhs_scale):
@@ -210,198 +203,114 @@ def tile_multigroup_neutron_source_s10_kernel(
                     stop=(g == PASSES - 1),
                 )
 
-        def scatter(u, side):
+        def scatter_columns(bank, u, side, first, width):
             h, m = divmod(u, M_TILES)
-            bank = psum.tile([P, BANK], F32, name="scatter_bank", bufs=4)
+            in_half = side * BANK + first
             product(
                 bank[:],
                 m,
-                lambda g: scat_codes[2 * h + side][:, g, :].bitcast(FP4X4),
-                lambda g: scat_plane[h][:, g, side * BANK : (side + 1) * BANK],
+                lambda g: scat_codes[2 * h + side][:, g, 2 * first : 2 * (first + width)].bitcast(FP4X4),
+                lambda g: scat_plane[h][:, g, in_half : in_half + width],
             )
-            if (u, side) in POOL_SIDES:
-                scatter_rows[u] = stream.tile([P, BANK], F32, name="scatter_rows", bufs=8)
-                nc.scalar.copy(out=scatter_rows[u][:], in_=bank[:])
-            scatter_bank[u, side] = bank
 
-        def delayed_rates(u):
+        def scatter(u, side):
+            bank = side_bank([P, BANK])
+            scatter_columns(bank, u, side, 0, BANK)
+            if u in GPSIMD_UNITS and side == 0:
+                rows = stream.tile([P, BANK], F32, name="scatter_rows", bufs=len(GPSIMD_UNITS))
+                nc.scalar.copy(out=rows[:], in_=bank[:])
+                scatter_sums[u, side] = rows
+            else:
+                scatter_sums[u, side] = bank
+
+        def rates(u):
             h, m = divmod(u, M_TILES)
-            fission_bank[u] = psum.tile([P, 2, R_HALF], F32, name="fission_bank", bufs=2)
+            bank = rate_bank([P, 2, R_HALF])
             product(
-                fission_bank[u][:, 1, :],
+                bank[:, 1, :],
                 m,
                 lambda g: delayed_codes[h][:, g * R_HALF : (g + 1) * R_HALF].bitcast(FP8X4),
                 lambda g: delayed_plane[h][:, g * R_HALF : (g + 1) * R_HALF],
             )
-
-        def prompt_rates(u):
-            h, m = divmod(u, M_TILES)
             product(
-                fission_bank[u][:, 0, :],
+                bank[:, 0, :],
                 m,
                 lambda g: prompt_codes[h][:, g, :].bitcast(FP8X4),
                 lambda g: prompt_plane[4 * g : P, h * R_HALF : (h + 1) * R_HALF],
             )
+            return bank
 
-        def spread_rates(u, i):
-            term = stream.tile([P, N_HALF], F32, name="term", bufs=6)
+        def multiply_spectra(u, bank):
+            terms = stream.tile([P, 2, N_HALF], F32, name="terms", bufs=3)
             nc.vector.tensor_tensor(
-                out=term[:].rearrange("p (r b) -> p r b", b=B),
-                in0=fission_bank[u][:, i, :].unsqueeze(2).to_broadcast([P, R_HALF, B]),
-                in1=chi_rows[u // M_TILES][:, i, :].rearrange("p (r b) -> p r b", b=B),
+                out=terms[:].rearrange("p i (r b) -> p (i r) b", b=B),
+                in0=bank[:].rearrange("p i r -> p (i r)").unsqueeze(2).to_broadcast([P, 2 * R_HALF, B]),
+                in1=chi_rows[u // M_TILES][:].rearrange("p i (r b) -> p (i r) b", b=B),
                 op=MULT,
             )
-            fission_terms[u, i] = term
+            fission_terms[u] = terms
 
         def add_terms(u):
             both = stream.tile([P, N_HALF], F32, name="both", bufs=6)
-            nc.gpsimd.tensor_tensor(out=both[:], in0=fission_terms[u, 0][:], in1=fission_terms[u, 1][:], op=ADD)
+            width = BANK if u == UNITS - 1 else N_HALF
+            for first in range(0, N_HALF, width):
+                cols = slice(first, first + width)
+                nc.gpsimd.tensor_tensor(
+                    out=both[:, cols], in0=fission_terms[u][:, 0, cols], in1=fission_terms[u][:, 1, cols], op=ADD
+                )
             fission_sum[u] = both
 
-        def finish(u, side):
+        def add_and_store(engine, sums, u, in_half, width):
             h, m = divmod(u, M_TILES)
-            result = stream.tile([P, BANK], F32, name="result", bufs=10)
-            cols = slice(side * BANK, (side + 1) * BANK)
-            if (u, side) in POOL_SIDES:
-                nc.gpsimd.tensor_tensor(out=result[:], in0=scatter_rows[u][:], in1=fission_sum[u][:, cols], op=ADD)
-            else:
-                nc.vector.tensor_tensor(out=result[:], in0=scatter_bank[u, side][:], in1=fission_sum[u][:, cols], op=ADD)
-            first = h * N_HALF + side * BANK
-            nc.sync.dma_start(out=out[m * P : (m + 1) * P, first : first + BANK], in_=result[:])
+            result = stream.tile([P, width], F32, name="result", bufs=10)
+            engine.tensor_tensor(out=result[:], in0=sums[:], in1=fission_sum[u][:, in_half : in_half + width], op=ADD)
+            column = h * N_HALF + in_half
+            nc.sync.dma_start(out=out[m * P : (m + 1) * P, column : column + width], in_=result[:])
+
+        def finish(u, side):
+            engine = nc.gpsimd if u in GPSIMD_UNITS and side == 0 else nc.vector
+            add_and_store(engine, scatter_sums[u, side], u, side * BANK, BANK)
 
         spread_chi(0)
         turn_flux(0)
-        quantize_flux(0, 1)
-        quantize_flux(1, 1)
         group_delayed(0, 0, nc.vector.tensor_copy)
-        turn_flux(1)
-        quantize_delayed(0, 0, 1)
-        quantize_flux(2, 2)
         group_delayed(0, 1, nc.vector.tensor_copy)
-        turn_flux(2)
-        quantize_delayed(0, 1, 1)
-        quantize_flux(4, 2)
-        group_delayed(0, 2, nc.vector.tensor_copy)
-        turn_flux(3)
-        quantize_delayed(0, 2, 1)
-        group_delayed(0, 3, nc.vector.tensor_copy)
-        quantize_flux(6, 2)
-        quantize_delayed(0, 3, 1)
-        delayed_rates(0)
-        prompt_rates(0)
-        spread_rates(0, 0)
-        spread_rates(0, 1)
-        add_terms(0)
-        delayed_rates(1)
-        prompt_rates(1)
-        turn_flux(4)
-        scatter(0, 0)
-        spread_rates(1, 0)
-        spread_rates(1, 1)
-        quantize_flux(8, 2)
-        add_terms(1)
-        delayed_rates(2)
-        prompt_rates(2)
-        turn_flux(5)
-        group_delayed(1, 0, nc.scalar.copy)
-        group_delayed(1, 1, nc.scalar.copy)
-        scatter(0, 1)
-        spread_rates(2, 0)
-        spread_rates(2, 1)
-        quantize_flux(10, 2)
-        add_terms(2)
-        finish(0, 0)
-        finish(0, 1)
-        delayed_rates(3)
-        prompt_rates(3)
         spread_chi(1)
-        group_delayed(1, 2, nc.scalar.copy)
-        group_delayed(1, 3, nc.scalar.copy)
-        scatter(1, 0)
-        scatter(1, 1)
-        spread_rates(3, 0)
-        spread_rates(3, 1)
-        add_terms(3)
-        finish(1, 0)
-        finish(1, 1)
-        delayed_rates(4)
-        prompt_rates(4)
-        scatter(2, 0)
-        scatter(2, 1)
-        spread_rates(4, 0)
-        spread_rates(4, 1)
-        quantize_delayed(1, 0, 4)
-        add_terms(4)
-        finish(2, 0)
-        finish(2, 1)
-        delayed_rates(5)
-        prompt_rates(5)
-        scatter(3, 0)
-        scatter(3, 1)
-        spread_rates(5, 0)
-        spread_rates(5, 1)
-        add_terms(5)
-        finish(3, 0)
-        finish(3, 1)
-        delayed_rates(6)
-        prompt_rates(6)
-        scatter(4, 0)
-        scatter(4, 1)
-        spread_rates(6, 0)
-        spread_rates(6, 1)
-        add_terms(6)
-        finish(4, 0)
-        finish(4, 1)
-        delayed_rates(7)
-        prompt_rates(7)
-        scatter(5, 0)
-        scatter(5, 1)
-        spread_rates(7, 0)
-        spread_rates(7, 1)
-        add_terms(7)
-        finish(5, 0)
-        finish(5, 1)
-        delayed_rates(8)
-        prompt_rates(8)
-        scatter(6, 0)
-        scatter(6, 1)
-        spread_rates(8, 0)
-        spread_rates(8, 1)
-        add_terms(8)
-        finish(6, 0)
-        finish(6, 1)
-        delayed_rates(9)
-        prompt_rates(9)
-        scatter(7, 0)
-        scatter(7, 1)
-        spread_rates(9, 0)
-        spread_rates(9, 1)
-        add_terms(9)
-        finish(7, 0)
-        finish(7, 1)
-        delayed_rates(10)
-        prompt_rates(10)
-        scatter(8, 0)
-        scatter(8, 1)
-        spread_rates(10, 0)
-        spread_rates(10, 1)
-        add_terms(10)
-        finish(8, 0)
-        finish(8, 1)
-        delayed_rates(11)
-        prompt_rates(11)
-        scatter(9, 0)
-        scatter(9, 1)
-        spread_rates(11, 0)
-        spread_rates(11, 1)
-        add_terms(11)
-        finish(9, 0)
-        finish(9, 1)
-        scatter(10, 0)
-        scatter(10, 1)
-        scatter(11, 0)
-        scatter(11, 1)
-        finish(10, 0)
-        finish(10, 1)
-        finish(11, 0)
-        finish(11, 1)
+        quantize_flux(0)
+        turn_flux(1)
+        quantize_delayed(0, 0, 2)
+        group_delayed(0, 2, nc.vector.tensor_copy)
+        group_delayed(0, 3, nc.vector.tensor_copy)
+        quantize_delayed(0, 2, 1)
+        quantize_delayed(0, 3, 1)
+        quantize_flux(1)
+
+        for u in range(UNITS):
+            bank = rates(u)
+            if u + HEAD_TILES < M_TILES:
+                turn_flux(u + HEAD_TILES)
+            if u in DELAYED_STEPS:
+                for g in range(2):
+                    group_delayed(1, 2 * DELAYED_STEPS.index(u) + g, nc.scalar.copy)
+            if u >= LAG:
+                for side in range(2):
+                    scatter(u - LAG, side)
+            multiply_spectra(u, bank)
+            if u + HEAD_TILES < M_TILES:
+                quantize_flux(u + HEAD_TILES)
+            if u == DELAYED_STEPS[-1] + 1:
+                quantize_delayed(1, 0, PASSES)
+            add_terms(u)
+            if u >= LAG:
+                for side in range(2):
+                    finish(u - LAG, side)
+
+        last_sides = [(u, side) for u in range(UNITS - LAG, UNITS) for side in range(2)][:-1]
+        for u, side in last_sides:
+            scatter(u, side)
+        for u, side in last_sides:
+            finish(u, side)
+        for j in range(BANK // NARROW):
+            bank = (turn_bank, rate_bank)[j % 2]([P, NARROW])
+            scatter_columns(bank, UNITS - 1, 1, j * NARROW, NARROW)
+            add_and_store(nc.vector, bank, UNITS - 1, BANK + j * NARROW, NARROW)

@@ -26,8 +26,9 @@ UNITS = HALVES * M_TILES
 PASS_COLS = R_HALF * PACK
 HEAD_TILES = 2
 LAG = 2
-GPSIMD_UNITS = (1, 3, 5, 7)
+GPSIMD_UNITS = range(2, 8, 2)
 DELAYED_STEPS = (2, 3)
+SORT_IN_STEP = {0: 4, 2: 5}
 NARROW = BANK // 4
 
 FLOPS = 2 * M * K * (R * B + 2 * R)
@@ -116,11 +117,11 @@ def tile_multigroup_neutron_source_s10_kernel(
         load_prompt_codes(0)
         load_flux(2)
         load_flux(3)
-        load_scat_scales(0)
         load_flux(4)
+        load_scat_scales(0)
         load_scat_codes(0, 0)
-        load_flux(5)
         load_scat_codes(0, 1)
+        load_flux(5)
         load_delayed(1, range(PASSES))
         load_prompt_codes(1)
         load_scat_scales(1)
@@ -135,20 +136,31 @@ def tile_multigroup_neutron_source_s10_kernel(
         delayed_plane = [kept("delayed_plane%d" % h, [P, PASSES * R_HALF], U8) for h in range(HALVES)]
         chi_rows = [kept("chi_rows%d" % h, [P, 2, N_HALF], BF16) for h in range(HALVES)]
 
+        flux_sorted = {}
         scatter_sums = {}
         fission_terms = {}
         fission_sum = {}
 
+        def sort_flux(m):
+            ordered = kept("flux_sorted%d" % m, [P, K // 2], F32)
+            nc.scalar.copy(
+                out=ordered[:].rearrange("p (g e c) -> p g e c", g=PASSES, e=2),
+                in_=flux_rest[m][:].bitcast(F32).rearrange("p (g c e) -> p g e c", g=PASSES, e=2),
+            )
+            flux_sorted[m] = ordered
+
+        def parity_words(m, g, e):
+            if m in flux_sorted:
+                return flux_sorted[m][:, (2 * g + e) * P : (2 * g + e + 1) * P]
+            if m == 0:
+                return flux_first[g // 2][:].bitcast(F32)[:, 2 * P * (g % 2) + e : 2 * P * (g % 2 + 1) : 2]
+            return flux_rest[m][:].bitcast(F32)[:, 2 * P * g + e : 2 * P * (g + 1) : 2]
+
         def turn_flux(m):
             for pair in range(PASSES // 2):
                 bank = turn_bank([P, 4, P])
-                if m == 0:
-                    words = flux_first[pair][:].bitcast(F32)
-                else:
-                    words = flux_rest[m][:].bitcast(F32)[:, 4 * P * pair : 4 * P * (pair + 1)]
                 for i in range(4):
-                    g, e = divmod(i, 2)
-                    nc.tensor.transpose(bank[:, i, :], words[:, 2 * P * g + e : 2 * P * (g + 1) : 2], ident[:])
+                    nc.tensor.transpose(bank[:, i, :], parity_words(m, 2 * pair + i // 2, i % 2), ident[:])
                 first = m * K + pair * K // 2
                 nc.scalar.copy(
                     out=flux_grouped[:, first : first + K // 2].bitcast(F32).rearrange("p (g s e) -> p g s e", g=2, e=2),
@@ -271,8 +283,8 @@ def tile_multigroup_neutron_source_s10_kernel(
             engine = nc.gpsimd if u in GPSIMD_UNITS and side == 0 else nc.vector
             add_and_store(engine, scatter_sums[u, side], u, side * BANK, BANK)
 
-        spread_chi(0)
         turn_flux(0)
+        spread_chi(0)
         group_delayed(0, 0, nc.vector.tensor_copy)
         group_delayed(0, 1, nc.vector.tensor_copy)
         spread_chi(1)
@@ -289,6 +301,8 @@ def tile_multigroup_neutron_source_s10_kernel(
             bank = rates(u)
             if u + HEAD_TILES < M_TILES:
                 turn_flux(u + HEAD_TILES)
+            if u in SORT_IN_STEP:
+                sort_flux(SORT_IN_STEP[u])
             if u in DELAYED_STEPS:
                 for g in range(2):
                     group_delayed(1, 2 * DELAYED_STEPS.index(u) + g, nc.scalar.copy)

@@ -26,8 +26,8 @@ UNITS = HALVES * M_TILES
 PASS_COLS = R_HALF * PACK
 HEAD_TILES = 2
 LAG = 2
-GPSIMD_UNITS = range(2, 8, 2)
-DELAYED_STEPS = (2, 3)
+GPSIMD_UNITS = range(1, 9, 2)
+DELAYED_STEP = M_TILES - 1 - HEAD_TILES
 SORT_IN_STEP = {0: 4, 2: 5}
 NARROW = BANK // 4
 
@@ -262,8 +262,16 @@ def tile_multigroup_neutron_source_s10_kernel(
             )
             fission_terms[u] = terms
 
+        def sum_buffer(u):
+            if u + HEAD_TILES < M_TILES:
+                m = u + HEAD_TILES
+                return flux_grouped[:, m * K : (m + 1) * K].bitcast(F32)
+            if u == DELAYED_STEP + 1:
+                return delayed_grouped[1][:, : 2 * N_HALF].bitcast(F32)
+            return stream.tile([P, N_HALF], F32, name="both", bufs=4)[:]
+
         def add_terms(u):
-            both = stream.tile([P, N_HALF], F32, name="both", bufs=6)
+            both = sum_buffer(u)
             width = BANK if u == UNITS - 1 else N_HALF
             for first in range(0, N_HALF, width):
                 cols = slice(first, first + width)
@@ -303,16 +311,16 @@ def tile_multigroup_neutron_source_s10_kernel(
                 turn_flux(u + HEAD_TILES)
             if u in SORT_IN_STEP:
                 sort_flux(SORT_IN_STEP[u])
-            if u in DELAYED_STEPS:
-                for g in range(2):
-                    group_delayed(1, 2 * DELAYED_STEPS.index(u) + g, nc.scalar.copy)
+            if u == DELAYED_STEP:
+                for g in range(PASSES):
+                    group_delayed(1, g, nc.scalar.copy)
             if u >= LAG:
                 for side in range(2):
                     scatter(u - LAG, side)
             multiply_spectra(u, bank)
             if u + HEAD_TILES < M_TILES:
                 quantize_flux(u + HEAD_TILES)
-            if u == DELAYED_STEPS[-1] + 1:
+            if u == DELAYED_STEP + 1:
                 quantize_delayed(1, 0, PASSES)
             add_terms(u)
             if u >= LAG:

from contextlib import ExitStack

import concourse.mybir as mybir
from concourse.masks import make_identity

F32 = mybir.dt.float32
BF16 = mybir.dt.bfloat16
I32 = mybir.dt.int32
U32 = mybir.dt.uint32
U8 = mybir.dt.uint8
FP8X4 = mybir.dt.float8_e4m3fn_x4
FP4X4 = mybir.dt.float4_e2m1fn_x4
MULT = mybir.AluOpType.mult
ADD = mybir.AluOpType.add

M, K, R, B = 768, 2048, 512, 4
P = 128
PACK = 4
PASSES = K // (P * PACK)
M_TILES = M // P
HALVES = 2
R_HALF = R // HALVES
N_HALF = R_HALF * B
BANK = 512
UNITS = HALVES * M_TILES
PASS_COLS = R_HALF * PACK
HEAD_TILES = 2
LAG = 2
GPSIMD_UNITS = range(1, 9, 2)
DELAYED_STEP = M_TILES - 1 - HEAD_TILES
SORT_IN_STEP = {0: 4, 2: 5}
NARROW = BANK // 4

FLOPS = 2 * M * K * (R * B + 2 * R)


def tile_multigroup_neutron_source_s10_kernel(
    tc, flux, scat_words, scat_scales, prompt_words, prompt_scales, delayed, chi_prompt, chi_delayed, out
):
    nc = tc.nc
    with ExitStack() as ctx:
        keep = ctx.enter_context(tc.tile_pool(name="keep", bufs=1))
        stream = ctx.enter_context(tc.tile_pool(name="stream", bufs=2))
        psum = ctx.enter_context(tc.psum_pool(name="psum", bufs=2))
        ctx.enter_context(tc.manual_schedule())

        def kept(name, shape, dtype):
            return keep.tile(shape, dtype, name=name, align_bytes=64)

        def turn_bank(shape):
            return psum.tile(shape, F32, name="turn_bank", bufs=2)

        def rate_bank(shape):
            return psum.tile(shape, F32, name="rate_bank", bufs=2)

        def side_bank(shape):
            return psum.tile(shape, F32, name="side_bank", bufs=4)

        ident = kept("ident", [P, P], F32)
        make_identity(nc, ident[:])

        scat_plane = [kept("scat_plane%d" % h, [P, PASSES, N_HALF], U8) for h in range(HALVES)]
        prompt_plane = kept("prompt_plane", [P, R], U8)
        nc.vector.memset(scat_plane[0][:].rearrange("p g n -> p (g n)").bitcast(I32), 0)
        nc.vector.memset(prompt_plane[:].bitcast(I32), 0)
        nc.vector.memset(scat_plane[1][:].rearrange("p g n -> p (g n)").bitcast(I32), 0)

        flux_first = [kept("flux_first%d" % pair, [P, K // 2], BF16) for pair in range(2)]
        flux_rest = {m: kept("flux_rest%d" % m, [P, K], BF16) for m in range(1, M_TILES)}
        scat_codes = [kept("scat_codes%d" % c, [P, PASSES, 2 * BANK], U8) for c in range(2 * HALVES)]
        prompt_codes = [kept("prompt_codes%d" % h, [P, PASSES, R_HALF], U32) for h in range(HALVES)]
        delayed_raw = [
            [kept("delayed_raw%d_%d" % (h, g), [P, PACK, R_HALF], BF16) for g in range(PASSES)] for h in range(HALVES)
        ]
        chi_raw = [kept("chi_raw%d" % i, [P, HALVES, 2 * B], BF16) for i in range(2)]

        def load_flux(m):
            nc.sync.dma_start(out=flux_rest[m][:], in_=flux[m * P : (m + 1) * P, :])

        def load_scat_scales(h):
            rows = scat_scales.rearrange("g (q r) n -> r q g n", r=4)
            for r in range(4):
                nc.sync.dma_start(
                    out=scat_plane[h][r:P:32, :, :].bitcast(I32),
                    in_=rows[r][:, :, h * N_HALF : (h + 1) * N_HALF].bitcast(I32),
                )

        def load_scat_codes(h, side):
            c = 2 * h + side
            src = scat_words.rearrange("g p c -> p g c")[:, :, c * 2 * BANK : (c + 1) * 2 * BANK]
            nc.sync.dma_start(out=scat_codes[c][:].bitcast(I32), in_=src.bitcast(I32))

        def load_prompt_scales():
            for q in range(4):
                nc.sync.dma_start(
                    out=prompt_plane[32 * q : 32 * q + 16, :].bitcast(I32),
                    in_=prompt_scales[:, 4 * q : 4 * q + 4, :].bitcast(I32),
                )

        def load_prompt_codes(h):
            src = prompt_words.rearrange("g p n t -> p g (n t)")[:, :, h * PACK * R_HALF : (h + 1) * PACK * R_HALF]
            nc.sync.dma_start(out=prompt_codes[h][:].bitcast(I32), in_=src.bitcast(I32))

        def load_delayed(h, passes):
            for g in passes:
                rows = delayed[g * P * PACK : (g + 1) * P * PACK, h * R_HALF : (h + 1) * R_HALF]
                nc.sync.dma_start(out=delayed_raw[h][g][:], in_=rows.rearrange("(p t) w -> p t w", t=PACK))

        for i, chi in enumerate((chi_prompt, chi_delayed)):
            nc.scalar.dma_start(out=chi_raw[i][:], in_=chi.rearrange("(h p r) b -> p h (r b)", h=HALVES, r=2))
        for pair in range(2):
            nc.sync.dma_start(out=flux_first[pair][:], in_=flux[:P, pair * K // 2 : (pair + 1) * K // 2])
        load_delayed(0, (0, 1))
        load_flux(1)
        load_delayed(0, (2, 3))
        load_prompt_scales()
        load_prompt_codes(0)
        load_flux(2)
        load_flux(3)
        load_flux(4)
        load_scat_scales(0)
        load_scat_codes(0, 0)
        load_scat_codes(0, 1)
        load_flux(5)
        load_delayed(1, range(PASSES))
        load_prompt_codes(1)
        load_scat_scales(1)
        load_scat_codes(1, 0)
        load_scat_codes(1, 1)

        flux_grouped = kept("flux_grouped", [P, M_TILES * K], BF16)
        flux_codes = kept("flux_codes", [P, M_TILES * PASSES * P], U32)
        flux_plane = kept("flux_plane", [P, M_TILES * PASSES * P], U8)
        delayed_grouped = [kept("delayed_grouped%d" % h, [P, PASSES * PASS_COLS], BF16) for h in range(HALVES)]
        delayed_codes = [kept("delayed_codes%d" % h, [P, PASSES * R_HALF], U32) for h in range(HALVES)]
        delayed_plane = [kept("delayed_plane%d" % h, [P, PASSES * R_HALF], U8) for h in range(HALVES)]
        chi_rows = [kept("chi_rows%d" % h, [P, 2, N_HALF], BF16) for h in range(HALVES)]

        flux_sorted = {}
        scatter_sums = {}
        fission_terms = {}
        fission_sum = {}

        def sort_flux(m):
            ordered = kept("flux_sorted%d" % m, [P, K // 2], F32)
            nc.scalar.copy(
                out=ordered[:].rearrange("p (g e c) -> p g e c", g=PASSES, e=2),
                in_=flux_rest[m][:].bitcast(F32).rearrange("p (g c e) -> p g e c", g=PASSES, e=2),
            )
            flux_sorted[m] = ordered

        def parity_words(m, g, e):
            if m in flux_sorted:
                return flux_sorted[m][:, (2 * g + e) * P : (2 * g + e + 1) * P]
            if m == 0:
                return flux_first[g // 2][:].bitcast(F32)[:, 2 * P * (g % 2) + e : 2 * P * (g % 2 + 1) : 2]
            return flux_rest[m][:].bitcast(F32)[:, 2 * P * g + e : 2 * P * (g + 1) : 2]

        def turn_flux(m):
            for pair in range(PASSES // 2):
                bank = turn_bank([P, 4, P])
                for i in range(4):
                    nc.tensor.transpose(bank[:, i, :], parity_words(m, 2 * pair + i // 2, i % 2), ident[:])
                first = m * K + pair * K // 2
                nc.scalar.copy(
                    out=flux_grouped[:, first : first + K // 2].bitcast(F32).rearrange("p (g s e) -> p g s e", g=2, e=2),
                    in_=bank[:].rearrange("p (g e) s -> p g s e", e=2),
                )

        def quantize_flux(m):
            cols = slice(m * PASSES * P, (m + 1) * PASSES * P)
            nc.vector.quantize_mx(
                out=flux_codes[:, cols].bitcast(FP8X4),
                scales=flux_plane[:, cols],
                in_=flux_grouped[:, m * K : (m + 1) * K],
            )

        def spread_chi(h):
            for i in range(2):
                bank = side_bank([P, 4, P])
                words = chi_raw[i][:, h, :].bitcast(F32)
                for j in range(4):
                    nc.tensor.transpose(bank[:, j, :], words[:, j : j + 1].to_broadcast([P, P]), ident[:])
                nc.scalar.copy(
                    out=chi_rows[h][:, i, :].bitcast(F32).rearrange("p (c j) -> p c j", j=4),
                    in_=bank[:].rearrange("p j c -> p c j"),
                )

        def group_delayed(h, g, copy):
            copy(
                out=delayed_grouped[h][:, g * PASS_COLS : (g + 1) * PASS_COLS].rearrange(
                    "p (c i t) -> p c t i", i=4, t=PACK
                ),
                in_=delayed_raw[h][g][:].rearrange("p t (c i) -> p c t i", i=4),
            )

        def quantize_delayed(h, first, count):
            cols = slice(first * R_HALF, (first + count) * R_HALF)
            nc.vector.quantize_mx(
                out=delayed_codes[h][:, cols].bitcast(FP8X4),
                scales=delayed_plane[h][:, cols],
                in_=delayed_grouped[h][:, first * PASS_COLS : (first + count) * PASS_COLS],
            )

        def product(acc, m, rhs, rhs_scale):
            for g in range(PASSES):
                cols = slice((m * PASSES + g) * P, (m * PASSES + g + 1) * P)
                nc.tensor.matmul_mx(
                    out=acc,
                    lhsT=flux_codes[:, cols].bitcast(FP8X4),
                    lhsT_scale=flux_plane[:, cols],
                    rhs=rhs(g),
                    rhs_scale=rhs_scale(g),
                    start=(g == 0),
                    stop=(g == PASSES - 1),
                )

        def scatter_columns(bank, u, side, first, width):
            h, m = divmod(u, M_TILES)
            in_half = side * BANK + first
            product(
                bank[:],
                m,
                lambda g: scat_codes[2 * h + side][:, g, 2 * first : 2 * (first + width)].bitcast(FP4X4),
                lambda g: scat_plane[h][:, g, in_half : in_half + width],
            )

        def scatter(u, side):
            bank = side_bank([P, BANK])
            scatter_columns(bank, u, side, 0, BANK)
            if u in GPSIMD_UNITS and side == 0:
                rows = stream.tile([P, BANK], F32, name="scatter_rows", bufs=len(GPSIMD_UNITS))
                nc.scalar.copy(out=rows[:], in_=bank[:])
                scatter_sums[u, side] = rows
            else:
                scatter_sums[u, side] = bank

        def rates(u):
            h, m = divmod(u, M_TILES)
            bank = rate_bank([P, 2, R_HALF])
            product(
                bank[:, 1, :],
                m,
                lambda g: delayed_codes[h][:, g * R_HALF : (g + 1) * R_HALF].bitcast(FP8X4),
                lambda g: delayed_plane[h][:, g * R_HALF : (g + 1) * R_HALF],
            )
            product(
                bank[:, 0, :],
                m,
                lambda g: prompt_codes[h][:, g, :].bitcast(FP8X4),
                lambda g: prompt_plane[4 * g : P, h * R_HALF : (h + 1) * R_HALF],
            )
            return bank

        def multiply_spectra(u, bank):
            terms = stream.tile([P, 2, N_HALF], F32, name="terms", bufs=3)
            nc.vector.tensor_tensor(
                out=terms[:].rearrange("p i (r b) -> p (i r) b", b=B),
                in0=bank[:].rearrange("p i r -> p (i r)").unsqueeze(2).to_broadcast([P, 2 * R_HALF, B]),
                in1=chi_rows[u // M_TILES][:].rearrange("p i (r b) -> p (i r) b", b=B),
                op=MULT,
            )
            fission_terms[u] = terms

        def sum_buffer(u):
            if u + HEAD_TILES < M_TILES:
                m = u + HEAD_TILES
                return flux_grouped[:, m * K : (m + 1) * K].bitcast(F32)
            if u == DELAYED_STEP + 1:
                return delayed_grouped[1][:, : 2 * N_HALF].bitcast(F32)
            return stream.tile([P, N_HALF], F32, name="both", bufs=4)[:]

        def add_terms(u):
            both = sum_buffer(u)
            width = BANK if u == UNITS - 1 else N_HALF
            for first in range(0, N_HALF, width):
                cols = slice(first, first + width)
                nc.gpsimd.tensor_tensor(
                    out=both[:, cols], in0=fission_terms[u][:, 0, cols], in1=fission_terms[u][:, 1, cols], op=ADD
                )
            fission_sum[u] = both

        def add_and_store(engine, sums, u, in_half, width):
            h, m = divmod(u, M_TILES)
            result = stream.tile([P, width], F32, name="result", bufs=10)
            engine.tensor_tensor(out=result[:], in0=sums[:], in1=fission_sum[u][:, in_half : in_half + width], op=ADD)
            column = h * N_HALF + in_half
            nc.sync.dma_start(out=out[m * P : (m + 1) * P, column : column + width], in_=result[:])

        def finish(u, side):
            engine = nc.gpsimd if u in GPSIMD_UNITS and side == 0 else nc.vector
            add_and_store(engine, scatter_sums[u, side], u, side * BANK, BANK)

        turn_flux(0)
        spread_chi(0)
        group_delayed(0, 0, nc.vector.tensor_copy)
        group_delayed(0, 1, nc.vector.tensor_copy)
        spread_chi(1)
        quantize_flux(0)
        turn_flux(1)
        quantize_delayed(0, 0, 2)
        group_delayed(0, 2, nc.vector.tensor_copy)
        group_delayed(0, 3, nc.vector.tensor_copy)
        quantize_delayed(0, 2, 1)
        quantize_delayed(0, 3, 1)
        quantize_flux(1)

        for u in range(UNITS):
            bank = rates(u)
            if u + HEAD_TILES < M_TILES:
                turn_flux(u + HEAD_TILES)
            if u in SORT_IN_STEP:
                sort_flux(SORT_IN_STEP[u])
            if u == DELAYED_STEP:
                for g in range(PASSES):
                    group_delayed(1, g, nc.scalar.copy)
            if u >= LAG:
                for side in range(2):
                    scatter(u - LAG, side)
            multiply_spectra(u, bank)
            if u + HEAD_TILES < M_TILES:
                quantize_flux(u + HEAD_TILES)
            if u == DELAYED_STEP + 1:
                quantize_delayed(1, 0, PASSES)
            add_terms(u)
            if u >= LAG:
                for side in range(2):
                    finish(u - LAG, side)

        last_sides = [(u, side) for u in range(UNITS - LAG, UNITS) for side in range(2)][:-1]
        for u, side in last_sides:
            scatter(u, side)
        for u, side in last_sides:
            finish(u, side)
        for j in range(BANK // NARROW):
            bank = (turn_bank, rate_bank)[j % 2]([P, NARROW])
            scatter_columns(bank, UNITS - 1, 1, j * NARROW, NARROW)
            add_and_store(nc.vector, bank, UNITS - 1, BANK + j * NARROW, NARROW)
